import numpy as np
import ml_dtypes


def mxq(x, axis, fmt="e4m3"):
    dtype, down = {"e4m3": (ml_dtypes.float8_e4m3fn, 7), "e5m2": (ml_dtypes.float8_e5m2, 14)}[fmt]
    v = np.moveaxis(np.asarray(x, np.float32).astype(ml_dtypes.bfloat16).astype(np.float64), axis, -1)
    blocks = v.reshape(v.shape[:-1] + (-1, 32))
    amax = np.abs(blocks).max(-1, keepdims=True)
    byte = np.maximum(np.where(amax > 0, np.frexp(amax)[1] - 1 + 127, 0) - down, 1)
    scale = np.exp2(byte - 127.0)
    codes = (blocks / scale).astype(np.float32).astype(dtype).astype(np.float64)
    return np.moveaxis((codes * scale).reshape(v.shape), -1, axis)


WIDE = False


def mx_kscale(k):
    if not WIDE:
        return np.ones(k)
    levels = np.array([10, -10, 5, -5, 0])
    if k % 512:
        return np.exp2(np.random.permutation(np.resize(levels, k // 32))).repeat(32)
    a = np.empty((k // 512, 16))
    for p in range(k // 512):
        a[p, :8] = np.random.permutation(np.resize(levels, 8))
        for g in range(8):
            far = levels[np.abs(levels - a[p, g]) >= 10]
            a[p, g + 8] = far[np.random.randint(len(far))]
    return np.exp2(a.ravel()).repeat(32)


def f64(x):
    return np.asarray(x).astype(np.float64)


def striped(idx):
    return np.tile(idx.reshape(-1, 16).T, (8, 1)).astype(np.uint16)


def unstriped(offs):
    return offs[:16].T.reshape(-1).astype(np.int64)


def silu(v):
    return v / (1.0 + np.exp(-np.maximum(v, -700.0)))


K, T, E, C, H, N = 1536, 1536, 2, 256, 512, 384


def by_expert(wq, xq):
    return np.concatenate([wq[e].T @ xq[:, e * C:(e + 1) * C] for e in range(E)], axis=1)


def setup_inputs():
    n = np.random.standard_normal
    s = mx_kscale(K)[:, None]
    u = mx_kscale(H)
    return {
        "xT": (n((K, T)) * s).astype(np.float32),
        "w1": (n((E, K, H)) / np.sqrt(K) / s[None] * u[None, None, :]).astype(np.float32),
        "w2": (n((E, H, N)) / np.sqrt(H) / u[None, :, None]).astype(np.float32),
        "gate": np.tile(np.random.uniform(0.2, 1.0, E * C), (N, 1)).astype(np.float32),
        "offs": striped(np.random.permutation(T)[:E * C]),
    }


def reference(xT, w1, w2, gate, offs):
    idx = unstriped(offs)
    xq = mxq(f64(xT)[:, idx], 0, "e4m3")
    h = silu(by_expert(mxq(f64(w1), 1, "e4m3"), xq))
    y = by_expert(mxq(f64(w2), 1, "e4m3"), mxq(h, 0, "e4m3"))
    out = np.zeros((N, T))
    out[:, idx] = f64(gate) * y
    return out

@@ -1,0 +1,191 @@
+import concourse.mybir as mybir
+
+K, T, E, C, H, N = 1536, 1536, 2, 256, 512, 384
+P = 128
+J = 4
+K_PASS = P * J
+PASSES = K // K_PASS
+SLOTS = E * C
+HALF = 128
+FEATURE_BLOCKS = N // P
+
+FLOPS = 2 * SLOTS * (K * H + H * N)
+
+F32 = mybir.dt.float32
+BF16 = mybir.dt.bfloat16
+U8 = mybir.dt.uint8
+U16 = mybir.dt.uint16
+U32 = mybir.dt.uint32
+FP8X4 = mybir.dt.float8_e4m3fn_x4
+SILU = mybir.ActivationFunctionType.Silu
+MULT = mybir.AluOpType.mult
+
+
+def tile_routed_moe_kernel(tc, xT, w1, w2, gate, offs, out):
+    nc = tc.nc
+    with (
+        tc.tile_pool(name="keep", bufs=1) as keep,
+        tc.tile_pool(name="ring", bufs=2) as ring,
+        tc.psum_pool(name="psum", bufs=4) as psum,
+    ):
+        lists = keep.tile([P, SLOTS // 16], U16, name="lists")
+        nc.sync.dma_start(lists[:], offs)
+
+        warm = keep.tile([P, 1], F32, name="warm")
+        nc.gpsimd.memset(warm[:], 0.0)
+        warmed = keep.tile([P, 1], F32, name="warmed")
+        nc.scalar.activation(out=warmed[:], in_=warm[:], func=SILU)
+
+        windows = []
+        for n in range(FEATURE_BLOCKS):
+            window = keep.tile([P, T], F32, name=f"window{n}")
+            nc.vector.memset(window[:], 0.0)
+            windows.append(window)
+
+        def copy_on(engine, out, in_):
+            if engine == "scalar":
+                nc.scalar.copy(out=out, in_=in_)
+            else:
+                nc.vector.tensor_copy(out=out, in_=in_)
+
+        x_codes, x_scales = [], []
+        planes_of_pass = xT.rearrange("(g p t) n -> g p t n", p=P, t=J)
+
+        def tokens(g, engines):
+            gathered = ring.tile([P, J, SLOTS], F32, name="gathered")
+            for t in range(J):
+                plane = keep.tile([P, T], F32, name=f"plane{g}_{t}")
+                nc.sync.dma_start(plane[:], planes_of_pass[g, :, t, :])
+                nc.vector.tensor_copy(gathered[:, t, :], plane[:].indirect(lists[:]))
+            grouped = ring.tile([P, SLOTS, J], BF16, name="grouped", align_bytes=64)
+            codes = keep.tile([P, SLOTS], U32, name=f"x_codes{g}", align_bytes=64)
+            scales = keep.tile([P, SLOTS], U8, name=f"x_scales{g}", align_bytes=64)
+            width = SLOTS // len(engines)
+            for i, engine in enumerate(engines):
+                cols = slice(i * width, (i + 1) * width)
+                copy_on(
+                    engine,
+                    grouped[:, cols, :].rearrange("p (c i) t -> p c t i", i=4),
+                    gathered[:, :, cols].rearrange("p t (c i) -> p c t i", i=4),
+                )
+                nc.vector.quantize_mx(
+                    out=codes[:, cols].bitcast(FP8X4),
+                    scales=scales[:, cols],
+                    in_=grouped[:, cols, :].rearrange("p w j -> p (w j)"),
+                )
+            x_codes.append(codes)
+            x_scales.append(scales)
+
+        w1_quantised = {}
+
+        def first_weights(e, g, engine):
+            raw = keep.tile([P, J, H], F32, name=f"w1_raw{e}_{g}")
+            nc.sync.dma_start(raw[:], w1[e, g * K_PASS : (g + 1) * K_PASS, :].rearrange("(p j) c -> p j c", j=J))
+            grouped = ring.tile([P, H, J], BF16, name="w_grouped", bufs=3, align_bytes=64)
+            copy_on(
+                engine,
+                grouped[:].rearrange("p (t m) j -> p m j t", t=J),
+                raw[:].rearrange("p j (m t) -> p m j t", t=J),
+            )
+            codes = keep.tile([P, H], U32, name=f"w1_codes{e}_{g}", align_bytes=64)
+            scales = keep.tile([P, H], U8, name=f"w1_scales{e}_{g}", align_bytes=64)
+            nc.vector.quantize_mx(
+                out=codes[:].bitcast(FP8X4), scales=scales[:], in_=grouped[:].rearrange("p w j -> p (w j)")
+            )
+            w1_quantised[e, g] = (codes, scales)
+
+        w2_quantised = {}
+
+        def second_weights(e, engine):
+            raw = keep.tile([P, J, N], F32, name=f"w2_raw{e}")
+            nc.sync.dma_start(raw[:], w2[e].rearrange("(p j) c -> p j c", j=J))
+            codes = keep.tile([P, H], U32, name=f"w2_codes{e}", align_bytes=64)
+            scales = keep.tile([P, H], U8, name=f"w2_scales{e}", align_bytes=64)
+            grouped = ring.tile([P, H, J], BF16, name="w_grouped", bufs=3, align_bytes=64)
+            copy_on(
+                engine,
+                grouped[:, 0:N, :].rearrange("p (c i) t -> p c t i", i=4),
+                raw[:].rearrange("p t (c i) -> p c t i", i=4),
+            )
+            for lo, hi in ((0, 256), (256, 384)):
+                nc.vector.quantize_mx(
+                    out=codes[:, lo:hi].bitcast(FP8X4),
+                    scales=scales[:, lo:hi],
+                    in_=grouped[:, lo:hi, :].rearrange("p w j -> p (w j)"),
+                )
+            w2_quantised[e] = (codes, scales)
+
+        def expert(e):
+            hidden = []
+            for s in range(C // HALF):
+                slots = slice(e * C + s * HALF, e * C + (s + 1) * HALF)
+                acc = psum.tile([P, J, HALF], F32, name="hidden_acc")
+                for t in range(J):
+                    rows = slice(t * P, (t + 1) * P)
+                    for g in range(PASSES):
+                        codes, scales = w1_quantised[e, g]
+                        nc.tensor.matmul_mx(
+                            out=acc[:, t, :],
+                            lhsT=codes[:, rows].bitcast(FP8X4),
+                            lhsT_scale=scales[:, rows],
+                            rhs=x_codes[g][:, slots].bitcast(FP8X4),
+                            rhs_scale=x_scales[g][:, slots],
+                            start=(g == 0),
+                            stop=(g == PASSES - 1),
+                        )
+                grouped = ring.tile([P, HALF, J], BF16, name="h_grouped", bufs=4, align_bytes=64)
+                nc.scalar.activation(out=grouped[:], in_=acc[:].rearrange("p t n -> p n t"), func=SILU)
+                h_codes = ring.tile([P, HALF], U32, name="h_codes", bufs=4, align_bytes=64)
+                h_scales = ring.tile([P, HALF], U8, name="h_scales", bufs=4, align_bytes=64)
+                nc.vector.quantize_mx(
+                    out=h_codes[:].bitcast(FP8X4), scales=h_scales[:], in_=grouped[:].rearrange("p w j -> p (w j)")
+                )
+                hidden.append((h_codes, h_scales))
+            codes, scales = w2_quantised[e]
+            results = []
+            for n in range(FEATURE_BLOCKS):
+                rows = slice(n * P, (n + 1) * P)
+                acc = psum.tile([P, C], F32, name="result_acc")
+                for s, (h_codes, h_scales) in enumerate(hidden):
+                    nc.tensor.matmul_mx(
+                        out=acc[:, s * HALF : (s + 1) * HALF],
+                        lhsT=codes[:, rows].bitcast(FP8X4),
+                        lhsT_scale=scales[:, rows],
+                        rhs=h_codes[:].bitcast(FP8X4),
+                        rhs_scale=h_scales[:],
+                        start=True,
+                        stop=True,
+                    )
+                result = ring.tile([P, C], F32, name="result", bufs=6)
+                nc.scalar.copy(out=result[:], in_=acc[:])
+                results.append(result)
+            return results
+
+        def scatter(e, n, result):
+            nc.vector.tensor_tensor(
+                windows[n][:].indirect(lists[:, e * C // 16 : (e + 1) * C // 16]),
+                result[:],
+                gates[:, e * C : (e + 1) * C],
+                MULT,
+            )
+
+        tokens(0, ["scalar"])
+        first_weights(0, 0, "scalar")
+        tokens(1, ["scalar"])
+        first_weights(0, 1, "scalar")
+        first_weights(0, 2, "scalar")
+        tokens(2, ["scalar", "vector"])
+        second_weights(0, "scalar")
+        gates = keep.tile([P, SLOTS], F32, name="gates")
+        nc.sync.dma_start(gates[:], gate[0:P, :])
+        results0 = expert(0)
+        first_weights(1, 0, "scalar")
+        first_weights(1, 1, "scalar")
+        first_weights(1, 2, "scalar")
+        second_weights(1, "vector")
+        for n in range(FEATURE_BLOCKS):
+            scatter(0, n, results0[n])
+        results1 = expert(1)
+        for n in range(FEATURE_BLOCKS):
+            scatter(1, n, results1[n])
+            nc.sync.dma_start(out[n * P : (n + 1) * P, :], windows[n][:])

@@ -19,6 +19,7 @@ U32 = mybir.dt.uint32
 FP8X4 = mybir.dt.float8_e4m3fn_x4
 SILU = mybir.ActivationFunctionType.Silu
 MULT = mybir.AluOpType.mult
+ADD = mybir.AluOpType.add
 
 
 def tile_routed_moe_kernel(tc, xT, w1, w2, gate, offs, out):
@@ -30,12 +31,10 @@ def tile_routed_moe_kernel(tc, xT, w1, w2, gate, offs, out):
     ):
         lists = keep.tile([P, SLOTS // 16], U16, name="lists")
         nc.sync.dma_start(lists[:], offs)
-
         warm = keep.tile([P, 1], F32, name="warm")
         nc.gpsimd.memset(warm[:], 0.0)
         warmed = keep.tile([P, 1], F32, name="warmed")
         nc.scalar.activation(out=warmed[:], in_=warm[:], func=SILU)
-
         windows = []
         for n in range(FEATURE_BLOCKS):
             window = keep.tile([P, T], F32, name=f"window{n}")
@@ -43,21 +42,49 @@ def tile_routed_moe_kernel(tc, xT, w1, w2, gate, offs, out):
             windows.append(window)
 
         def copy_on(engine, out, in_):
-            if engine == "scalar":
+            if engine == "S":
                 nc.scalar.copy(out=out, in_=in_)
-            else:
+            elif engine == "V":
                 nc.vector.tensor_copy(out=out, in_=in_)
+            else:
+                nc.gpsimd.tensor_scalar(out=out, in0=in_, scalar1=1.0, scalar2=0.0, op0=MULT, op1=ADD)
 
-        x_codes, x_scales = [], []
         planes_of_pass = xT.rearrange("(g p t) n -> g p t n", p=P, t=J)
+        raws = {}
+        x_quantised = {}
 
-        def tokens(g, engines):
-            gathered = ring.tile([P, J, SLOTS], F32, name="gathered")
+        def load_plane(g, t):
+            raw = keep.tile([P, T], F32, name=f"plane{g}_{t}")
+            nc.sync.dma_start(raw[:], planes_of_pass[g, :, t, :])
+            raws["x", g, t] = raw
+
+        def load_pair(g, u, pieces):
+            raw = []
+            width = T // pieces
+            for h in range(pieces):
+                piece = keep.tile([P, 2, width], F32, name=f"planes{g}_{u}_{h}")
+                nc.sync.dma_start(piece[:], planes_of_pass[g, :, 2 * u : 2 * u + 2, h * width : (h + 1) * width])
+                raw.append(piece)
+            raws["x", g, u] = raw
+
+        def load_w1(e, g):
+            raw = keep.tile([P, J, H], F32, name=f"w1_raw{e}_{g}")
+            nc.sync.dma_start(raw[:], w1[e, g * K_PASS : (g + 1) * K_PASS, :].rearrange("(p j) c -> p j c", j=J))
+            raws["w1", e, g] = raw
+
+        def load_w2(e):
+            raw = keep.tile([P, J, N], F32, name=f"w2_raw{e}")
+            nc.sync.dma_start(raw[:], w2[e].rearrange("(p j) c -> p j c", j=J))
+            raws["w2", e] = raw
+
+        def quantise(codes, scales, grouped_columns):
+            nc.vector.quantize_mx(out=codes.bitcast(FP8X4), scales=scales, in_=grouped_columns)
+
+        def tokens_by_planes(g, engines):
+            gathered = ring.tile([P, J, SLOTS], F32, name="gathered", bufs=1)
             for t in range(J):
-                plane = keep.tile([P, T], F32, name=f"plane{g}_{t}")
-                nc.sync.dma_start(plane[:], planes_of_pass[g, :, t, :])
-                nc.vector.tensor_copy(gathered[:, t, :], plane[:].indirect(lists[:]))
-            grouped = ring.tile([P, SLOTS, J], BF16, name="grouped", align_bytes=64)
+                nc.vector.tensor_copy(gathered[:, t, :], raws["x", g, t][:].indirect(lists[:]))
+            grouped = ring.tile([P, SLOTS, J], BF16, name="grouped", bufs=1, align_bytes=64)
             codes = keep.tile([P, SLOTS], U32, name=f"x_codes{g}", align_bytes=64)
             scales = keep.tile([P, SLOTS], U8, name=f"x_scales{g}", align_bytes=64)
             width = SLOTS // len(engines)
@@ -68,81 +95,90 @@ def tile_routed_moe_kernel(tc, xT, w1, w2, gate, offs, out):
                     grouped[:, cols, :].rearrange("p (c i) t -> p c t i", i=4),
                     gathered[:, :, cols].rearrange("p t (c i) -> p c t i", i=4),
                 )
-                nc.vector.quantize_mx(
-                    out=codes[:, cols].bitcast(FP8X4),
-                    scales=scales[:, cols],
-                    in_=grouped[:, cols, :].rearrange("p w j -> p (w j)"),
-                )
-            x_codes.append(codes)
-            x_scales.append(scales)
+                quantise(codes[:, cols], scales[:, cols], grouped[:, cols, :].rearrange("p w j -> p (w j)"))
+            x_quantised[g] = (codes, scales)
+
+        def tokens_by_pairs(g, parts):
+            grouped = ring.tile([P, SLOTS, J // 2], U32, name="grouped_words", bufs=2, align_bytes=64)
+            for u in range(J // 2):
+                pairs = ring.tile([P, T], U32, name="pairs", bufs=2)
+                start = 0
+                for raw in raws["x", g, u]:
+                    for engine, lo, hi in parts[u]:
+                        copy_on(
+                            engine,
+                            pairs[:, start + lo : start + hi].bitcast(BF16).rearrange("p (c i u) -> p c u i", i=4, u=2),
+                            raw[:, :, lo:hi].rearrange("p u (c i) -> p c u i", i=4),
+                        )
+                    start += hi
+                nc.vector.tensor_copy(grouped[:, :, u], pairs[:].indirect(lists[:]))
+            codes = keep.tile([P, SLOTS], U32, name=f"x_codes{g}", align_bytes=64)
+            scales = keep.tile([P, SLOTS], U8, name=f"x_scales{g}", align_bytes=64)
+            quantise(codes[:], scales[:], grouped[:].rearrange("p w u -> p (w u)").bitcast(BF16))
+            x_quantised[g] = (codes, scales)
 
         w1_quantised = {}
 
-        def first_weights(e, g, engine):
-            raw = keep.tile([P, J, H], F32, name=f"w1_raw{e}_{g}")
-            nc.sync.dma_start(raw[:], w1[e, g * K_PASS : (g + 1) * K_PASS, :].rearrange("(p j) c -> p j c", j=J))
+        def first_weights(e, g, parts):
+            raw = raws["w1", e, g]
             grouped = ring.tile([P, H, J], BF16, name="w_grouped", bufs=3, align_bytes=64)
-            copy_on(
-                engine,
-                grouped[:].rearrange("p (t m) j -> p m j t", t=J),
-                raw[:].rearrange("p j (m t) -> p m j t", t=J),
-            )
+            for engine, lo, hi in parts:
+                copy_on(
+                    engine,
+                    grouped[:].rearrange("p (t m) j -> p m j t", t=J)[:, lo:hi, :, :],
+                    raw[:].rearrange("p j (m t) -> p m j t", t=J)[:, lo:hi, :, :],
+                )
             codes = keep.tile([P, H], U32, name=f"w1_codes{e}_{g}", align_bytes=64)
             scales = keep.tile([P, H], U8, name=f"w1_scales{e}_{g}", align_bytes=64)
-            nc.vector.quantize_mx(
-                out=codes[:].bitcast(FP8X4), scales=scales[:], in_=grouped[:].rearrange("p w j -> p (w j)")
-            )
+            quantise(codes[:], scales[:], grouped[:].rearrange("p w j -> p (w j)"))
             w1_quantised[e, g] = (codes, scales)
 
         w2_quantised = {}
 
-        def second_weights(e, engine):
-            raw = keep.tile([P, J, N], F32, name=f"w2_raw{e}")
-            nc.sync.dma_start(raw[:], w2[e].rearrange("(p j) c -> p j c", j=J))
-            codes = keep.tile([P, H], U32, name=f"w2_codes{e}", align_bytes=64)
-            scales = keep.tile([P, H], U8, name=f"w2_scales{e}", align_bytes=64)
+        def second_weights(e, parts):
+            raw = raws["w2", e]
+            codes = keep.tile([P, N], U32, name=f"w2_codes{e}", align_bytes=64)
+            scales = keep.tile([P, N], U8, name=f"w2_scales{e}", align_bytes=64)
             grouped = ring.tile([P, H, J], BF16, name="w_grouped", bufs=3, align_bytes=64)
-            copy_on(
-                engine,
-                grouped[:, 0:N, :].rearrange("p (c i) t -> p c t i", i=4),
-                raw[:].rearrange("p t (c i) -> p c t i", i=4),
-            )
-            for lo, hi in ((0, 256), (256, 384)):
-                nc.vector.quantize_mx(
-                    out=codes[:, lo:hi].bitcast(FP8X4),
-                    scales=scales[:, lo:hi],
-                    in_=grouped[:, lo:hi, :].rearrange("p w j -> p (w j)"),
+            for engine, lo, hi in parts:
+                copy_on(
+                    engine,
+                    grouped[:, lo:hi, :].rearrange("p (c i) t -> p c t i", i=4),
+                    raw[:, :, lo:hi].rearrange("p t (c i) -> p c t i", i=4),
                 )
+            for lo, hi in ((0, 256), (256, 384)):
+                quantise(codes[:, lo:hi], scales[:, lo:hi], grouped[:, lo:hi, :].rearrange("p w j -> p (w j)"))
             w2_quantised[e] = (codes, scales)
+
+        results = {}
 
         def expert(e):
             hidden = []
             for s in range(C // HALF):
                 slots = slice(e * C + s * HALF, e * C + (s + 1) * HALF)
-                acc = psum.tile([P, J, HALF], F32, name="hidden_acc")
-                for t in range(J):
-                    rows = slice(t * P, (t + 1) * P)
-                    for g in range(PASSES):
-                        codes, scales = w1_quantised[e, g]
-                        nc.tensor.matmul_mx(
-                            out=acc[:, t, :],
-                            lhsT=codes[:, rows].bitcast(FP8X4),
-                            lhsT_scale=scales[:, rows],
-                            rhs=x_codes[g][:, slots].bitcast(FP8X4),
-                            rhs_scale=x_scales[g][:, slots],
-                            start=(g == 0),
-                            stop=(g == PASSES - 1),
-                        )
                 grouped = ring.tile([P, HALF, J], BF16, name="h_grouped", bufs=4, align_bytes=64)
-                nc.scalar.activation(out=grouped[:], in_=acc[:].rearrange("p t n -> p n t"), func=SILU)
+                for q in range(0, J, 2):
+                    acc = psum.tile([P, 2, HALF], F32, name="hidden_acc")
+                    for t in range(q, q + 2):
+                        rows = slice(t * P, (t + 1) * P)
+                        for i, g in enumerate([[0,2,1],[0,2,1]][e]):
+                            codes, scales = w1_quantised[e, g]
+                            x_codes, x_scales = x_quantised[g]
+                            nc.tensor.matmul_mx(
+                                out=acc[:, t - q, :],
+                                lhsT=codes[:, rows].bitcast(FP8X4),
+                                lhsT_scale=scales[:, rows],
+                                rhs=x_codes[:, slots].bitcast(FP8X4),
+                                rhs_scale=x_scales[:, slots],
+                                start=(i == 0),
+                                stop=(i == PASSES - 1),
+                            )
+                    nc.scalar.activation(out=grouped[:, :, q : q + 2], in_=acc[:].rearrange("p t n -> p n t"), func=SILU)
                 h_codes = ring.tile([P, HALF], U32, name="h_codes", bufs=4, align_bytes=64)
                 h_scales = ring.tile([P, HALF], U8, name="h_scales", bufs=4, align_bytes=64)
-                nc.vector.quantize_mx(
-                    out=h_codes[:].bitcast(FP8X4), scales=h_scales[:], in_=grouped[:].rearrange("p w j -> p (w j)")
-                )
+                quantise(h_codes[:], h_scales[:], grouped[:].rearrange("p w j -> p (w j)"))
                 hidden.append((h_codes, h_scales))
             codes, scales = w2_quantised[e]
-            results = []
             for n in range(FEATURE_BLOCKS):
                 rows = slice(n * P, (n + 1) * P)
                 acc = psum.tile([P, C], F32, name="result_acc")
@@ -158,34 +194,47 @@ def tile_routed_moe_kernel(tc, xT, w1, w2, gate, offs, out):
                     )
                 result = ring.tile([P, C], F32, name="result", bufs=6)
                 nc.scalar.copy(out=result[:], in_=acc[:])
-                results.append(result)
-            return results
+                results[e, n] = result
 
-        def scatter(e, n, result):
-            nc.vector.tensor_tensor(
-                windows[n][:].indirect(lists[:, e * C // 16 : (e + 1) * C // 16]),
-                result[:],
-                gates[:, e * C : (e + 1) * C],
-                MULT,
-            )
+        def scatter(e):
+            for n in range(FEATURE_BLOCKS):
+                nc.vector.tensor_tensor(
+                    windows[n][:].indirect(lists[:, e * C // 16 : (e + 1) * C // 16]),
+                    results[e, n][:],
+                    gates[:, e * C : (e + 1) * C],
+                    MULT,
+                )
 
-        tokens(0, ["scalar"])
-        first_weights(0, 0, "scalar")
-        tokens(1, ["scalar"])
-        first_weights(0, 1, "scalar")
-        first_weights(0, 2, "scalar")
-        tokens(2, ["scalar", "vector"])
-        second_weights(0, "scalar")
         gates = keep.tile([P, SLOTS], F32, name="gates")
+        load_pair(0, 0, 2)
+        load_pair(0, 1, 2)
+        load_w1(0, 0)
+        load_pair(1, 0, 2)
+        load_pair(1, 1, 2)
+        load_pair(2, 0, 2)
+        load_pair(2, 1, 2)
+        load_w1(0, 2)
+        load_w1(0, 1)
+        load_w1(1, 0)
+        load_w2(0)
+        load_w1(1, 2)
+        load_w1(1, 1)
         nc.sync.dma_start(gates[:], gate[0:P, :])
-        results0 = expert(0)
-        first_weights(1, 0, "scalar")
-        first_weights(1, 1, "scalar")
-        first_weights(1, 2, "scalar")
-        second_weights(1, "vector")
+        load_w2(1)
+        first_weights(0, 2, [["S",0,48],["V",48,128]])
+        tokens_by_pairs(0, ([["S",0,480],["V",480,768]], [["S",0,192],["V",192,768]]))
+        first_weights(0, 0, [["S",0,128]])
+        first_weights(0, 1, [["S",0,48],["S",48,96],["V",96,128]])
+        second_weights(0, [["S",0,96],["V",96,384]])
+        first_weights(1, 0, [["S",0,48],["S",48,96],["V",96,128]])
+        tokens_by_pairs(1, ([["S",0,192],["S",192,384],["V",384,768]], [["S",0,480],["V",480,768]]))
+        tokens_by_pairs(2, ([["S",0,576],["V",576,768]], [["S",0,480],["V",480,768]]))
+        first_weights(1, 1, [["S",0,96],["V",96,128]])
+        second_weights(1, [["S",0,144],["V",144,384]])
+        first_weights(1, 2, [["V",0,128]])
+        expert(0)
+        expert(1)
+        scatter(0)
+        scatter(1)
         for n in range(FEATURE_BLOCKS):
-            scatter(0, n, results0[n])
-        results1 = expert(1)
-        for n in range(FEATURE_BLOCKS):
-            scatter(1, n, results1[n])
             nc.sync.dma_start(out[n * P : (n + 1) * P, :], windows[n][:])

@@ -161,7 +161,7 @@ def tile_routed_moe_kernel(tc, xT, w1, w2, gate, offs, out):
                     acc = psum.tile([P, 2, HALF], F32, name="hidden_acc")
                     for t in range(q, q + 2):
                         rows = slice(t * P, (t + 1) * P)
-                        for i, g in enumerate([[0,2,1],[0,2,1]][e]):
+                        for i, g in enumerate([[0,1,2],[0,1,2]][e]):
                             codes, scales = w1_quantised[e, g]
                             x_codes, x_scales = x_quantised[g]
                             nc.tensor.matmul_mx(
@@ -206,33 +206,35 @@ def tile_routed_moe_kernel(tc, xT, w1, w2, gate, offs, out):
                 )
 
         gates = keep.tile([P, SLOTS], F32, name="gates")
-        load_pair(0, 0, 2)
-        load_pair(0, 1, 2)
+        load_plane(0, 0)
+        load_plane(0, 1)
+        load_plane(0, 2)
+        load_plane(0, 3)
+        load_pair(1, 0, 1)
+        load_pair(1, 1, 1)
+        load_pair(2, 0, 1)
+        load_pair(2, 1, 1)
         load_w1(0, 0)
-        load_pair(1, 0, 2)
-        load_pair(1, 1, 2)
-        load_pair(2, 0, 2)
-        load_pair(2, 1, 2)
-        load_w1(0, 2)
         load_w1(0, 1)
-        load_w1(1, 0)
+        load_w1(0, 2)
         load_w2(0)
-        load_w1(1, 2)
+        load_w1(1, 0)
         load_w1(1, 1)
+        load_w1(1, 2)
         nc.sync.dma_start(gates[:], gate[0:P, :])
         load_w2(1)
-        first_weights(0, 2, [["S",0,48],["V",48,128]])
-        tokens_by_pairs(0, ([["S",0,480],["V",480,768]], [["S",0,192],["V",192,768]]))
-        first_weights(0, 0, [["S",0,128]])
-        first_weights(0, 1, [["S",0,48],["S",48,96],["V",96,128]])
-        second_weights(0, [["S",0,96],["V",96,384]])
-        first_weights(1, 0, [["S",0,48],["S",48,96],["V",96,128]])
-        tokens_by_pairs(1, ([["S",0,192],["S",192,384],["V",384,768]], [["S",0,480],["V",480,768]]))
-        tokens_by_pairs(2, ([["S",0,576],["V",576,768]], [["S",0,480],["V",480,768]]))
-        first_weights(1, 1, [["S",0,96],["V",96,128]])
-        second_weights(1, [["S",0,144],["V",144,384]])
-        first_weights(1, 2, [["V",0,128]])
+        tokens_by_planes(0, ["V","S"])
+        tokens_by_pairs(1, ([["S",0,768],["V",768,1536]], [["S",0,576],["V",576,1536]]))
+        tokens_by_pairs(2, ([["S",0,576],["V",576,1536]], [["S",0,960],["V",960,1536]]))
+        first_weights(0, 0, [["S",0,64],["S",64,128]])
+        first_weights(0, 1, [["S",0,64],["V",64,128]])
+        first_weights(0, 2, [["S",0,64],["V",64,128]])
+        second_weights(0, [["V",0,384]])
         expert(0)
+        first_weights(1, 0, [["V",0,128]])
+        first_weights(1, 1, [["S",0,48],["V",48,128]])
+        first_weights(1, 2, [["S",0,48],["V",48,128]])
+        second_weights(1, [["S",0,96],["V",96,384]])
         expert(1)
         scatter(0)
         scatter(1)

@@ -206,10 +206,8 @@ def tile_routed_moe_kernel(tc, xT, w1, w2, gate, offs, out):
                 )
 
         gates = keep.tile([P, SLOTS], F32, name="gates")
-        load_plane(0, 0)
-        load_plane(0, 1)
-        load_plane(0, 2)
-        load_plane(0, 3)
+        load_pair(0, 0, 1)
+        load_pair(0, 1, 1)
         load_pair(1, 0, 1)
         load_pair(1, 1, 1)
         load_pair(2, 0, 1)
@@ -223,18 +221,18 @@ def tile_routed_moe_kernel(tc, xT, w1, w2, gate, offs, out):
         load_w1(1, 2)
         nc.sync.dma_start(gates[:], gate[0:P, :])
         load_w2(1)
-        tokens_by_planes(0, ["V","S"])
-        tokens_by_pairs(1, ([["S",0,768],["V",768,1536]], [["S",0,576],["V",576,1536]]))
-        tokens_by_pairs(2, ([["S",0,576],["V",576,1536]], [["S",0,960],["V",960,1536]]))
-        first_weights(0, 0, [["S",0,64],["S",64,128]])
+        tokens_by_pairs(0, ([["S",0,768],["V",768,1536]], [["S",0,768],["V",768,1536]]))
+        tokens_by_pairs(1, ([["S",0,768],["V",768,1536]], [["S",0,768],["V",768,1536]]))
+        tokens_by_pairs(2, ([["S",0,768],["V",768,1536]], [["S",0,768],["V",768,1536]]))
+        first_weights(0, 0, [["S",0,128]])
         first_weights(0, 1, [["S",0,64],["V",64,128]])
         first_weights(0, 2, [["S",0,64],["V",64,128]])
         second_weights(0, [["V",0,384]])
         expert(0)
         first_weights(1, 0, [["V",0,128]])
-        first_weights(1, 1, [["S",0,48],["V",48,128]])
-        first_weights(1, 2, [["S",0,48],["V",48,128]])
-        second_weights(1, [["S",0,96],["V",96,384]])
+        first_weights(1, 1, [["S",0,32],["V",32,128]])
+        first_weights(1, 2, [["S",0,128]])
+        second_weights(1, [["V",0,384]])
         expert(1)
         scatter(0)
         scatter(1)

@@ -201,11 +201,18 @@ def tile_routed_moe_kernel(tc, xT, w1, w2, gate, offs, out):
                 nc.vector.tensor_tensor(
                     windows[n][:].indirect(lists[:, e * C // 16 : (e + 1) * C // 16]),
                     results[e, n][:],
-                    gates[:, e * C : (e + 1) * C],
+                    gates[n][:, e * C : (e + 1) * C],
                     MULT,
                 )
 
-        gates = keep.tile([P, SLOTS], F32, name="gates")
+        gates = []
+        for n in range(FEATURE_BLOCKS):
+            gate_rows = keep.tile([P, SLOTS], F32, name=f"gates{n}")
+            gates.append(gate_rows)
+
+        def load_gate(n):
+            nc.sync.dma_start(gates[n][:], gate[n * P : (n + 1) * P, :])
+
         load_pair(0, 0, 1)
         load_pair(0, 1, 1)
         load_pair(1, 0, 1)
@@ -217,10 +224,12 @@ def tile_routed_moe_kernel(tc, xT, w1, w2, gate, offs, out):
         load_w1(0, 2)
         load_w2(0)
         load_w1(1, 0)
+        load_gate(0)
         load_w1(1, 1)
+        load_gate(1)
         load_w1(1, 2)
-        nc.sync.dma_start(gates[:], gate[0:P, :])
         load_w2(1)
+        load_gate(2)
         tokens_by_pairs(0, ([["S",0,768],["V",768,1536]], [["S",0,768],["V",768,1536]]))
         tokens_by_pairs(1, ([["S",0,768],["V",768,1536]], [["S",0,768],["V",768,1536]]))
         tokens_by_pairs(2, ([["S",0,768],["V",768,1536]], [["S",0,768],["V",768,1536]]))
@@ -230,9 +239,9 @@ def tile_routed_moe_kernel(tc, xT, w1, w2, gate, offs, out):
         second_weights(0, [["V",0,384]])
         expert(0)
         first_weights(1, 0, [["V",0,128]])
-        first_weights(1, 1, [["S",0,32],["V",32,128]])
+        first_weights(1, 1, [["S",0,64],["V",64,128]])
         first_weights(1, 2, [["S",0,128]])
-        second_weights(1, [["V",0,384]])
+        second_weights(1, [["S",0,288],["V",288,384]])
         expert(1)
         scatter(0)
         scatter(1)

import concourse.mybir as mybir

K, T, E, C, H, N = 1536, 1536, 2, 256, 512, 384
P = 128
J = 4
K_PASS = P * J
PASSES = K // K_PASS
SLOTS = E * C
HALF = 128
FEATURE_BLOCKS = N // P

FLOPS = 2 * SLOTS * (K * H + H * N)

F32 = mybir.dt.float32
BF16 = mybir.dt.bfloat16
U8 = mybir.dt.uint8
U16 = mybir.dt.uint16
U32 = mybir.dt.uint32
FP8X4 = mybir.dt.float8_e4m3fn_x4
SILU = mybir.ActivationFunctionType.Silu
MULT = mybir.AluOpType.mult
ADD = mybir.AluOpType.add


def tile_routed_moe_kernel(tc, xT, w1, w2, gate, offs, out):
    nc = tc.nc
    with (
        tc.tile_pool(name="keep", bufs=1) as keep,
        tc.tile_pool(name="ring", bufs=2) as ring,
        tc.psum_pool(name="psum", bufs=4) as psum,
    ):
        lists = keep.tile([P, SLOTS // 16], U16, name="lists")
        nc.sync.dma_start(lists[:], offs)
        warm = keep.tile([P, 1], F32, name="warm")
        nc.gpsimd.memset(warm[:], 0.0)
        warmed = keep.tile([P, 1], F32, name="warmed")
        nc.scalar.activation(out=warmed[:], in_=warm[:], func=SILU)
        windows = []
        for n in range(FEATURE_BLOCKS):
            window = keep.tile([P, T], F32, name=f"window{n}")
            nc.vector.memset(window[:], 0.0)
            windows.append(window)

        def copy_on(engine, out, in_):
            if engine == "S":
                nc.scalar.copy(out=out, in_=in_)
            elif engine == "V":
                nc.vector.tensor_copy(out=out, in_=in_)
            else:
                nc.gpsimd.tensor_scalar(out=out, in0=in_, scalar1=1.0, scalar2=0.0, op0=MULT, op1=ADD)

        planes_of_pass = xT.rearrange("(g p t) n -> g p t n", p=P, t=J)
        raws = {}
        x_quantised = {}

        def load_plane(g, t):
            raw = keep.tile([P, T], F32, name=f"plane{g}_{t}")
            nc.sync.dma_start(raw[:], planes_of_pass[g, :, t, :])
            raws["x", g, t] = raw

        def load_pair(g, u, pieces):
            raw = []
            width = T // pieces
            for h in range(pieces):
                piece = keep.tile([P, 2, width], F32, name=f"planes{g}_{u}_{h}")
                nc.sync.dma_start(piece[:], planes_of_pass[g, :, 2 * u : 2 * u + 2, h * width : (h + 1) * width])
                raw.append(piece)
            raws["x", g, u] = raw

        def load_w1(e, g):
            raw = keep.tile([P, J, H], F32, name=f"w1_raw{e}_{g}")
            nc.sync.dma_start(raw[:], w1[e, g * K_PASS : (g + 1) * K_PASS, :].rearrange("(p j) c -> p j c", j=J))
            raws["w1", e, g] = raw

        def load_w2(e):
            raw = keep.tile([P, J, N], F32, name=f"w2_raw{e}")
            nc.sync.dma_start(raw[:], w2[e].rearrange("(p j) c -> p j c", j=J))
            raws["w2", e] = raw

        def quantise(codes, scales, grouped_columns):
            nc.vector.quantize_mx(out=codes.bitcast(FP8X4), scales=scales, in_=grouped_columns)

        def tokens_by_planes(g, engines):
            gathered = ring.tile([P, J, SLOTS], F32, name="gathered", bufs=1)
            for t in range(J):
                nc.vector.tensor_copy(gathered[:, t, :], raws["x", g, t][:].indirect(lists[:]))
            grouped = ring.tile([P, SLOTS, J], BF16, name="grouped", bufs=1, align_bytes=64)
            codes = keep.tile([P, SLOTS], U32, name=f"x_codes{g}", align_bytes=64)
            scales = keep.tile([P, SLOTS], U8, name=f"x_scales{g}", align_bytes=64)
            width = SLOTS // len(engines)
            for i, engine in enumerate(engines):
                cols = slice(i * width, (i + 1) * width)
                copy_on(
                    engine,
                    grouped[:, cols, :].rearrange("p (c i) t -> p c t i", i=4),
                    gathered[:, :, cols].rearrange("p t (c i) -> p c t i", i=4),
                )
                quantise(codes[:, cols], scales[:, cols], grouped[:, cols, :].rearrange("p w j -> p (w j)"))
            x_quantised[g] = (codes, scales)

        def tokens_by_pairs(g, parts):
            grouped = ring.tile([P, SLOTS, J // 2], U32, name="grouped_words", bufs=2, align_bytes=64)
            for u in range(J // 2):
                pairs = ring.tile([P, T], U32, name="pairs", bufs=2)
                start = 0
                for raw in raws["x", g, u]:
                    for engine, lo, hi in parts[u]:
                        copy_on(
                            engine,
                            pairs[:, start + lo : start + hi].bitcast(BF16).rearrange("p (c i u) -> p c u i", i=4, u=2),
                            raw[:, :, lo:hi].rearrange("p u (c i) -> p c u i", i=4),
                        )
                    start += hi
                nc.vector.tensor_copy(grouped[:, :, u], pairs[:].indirect(lists[:]))
            codes = keep.tile([P, SLOTS], U32, name=f"x_codes{g}", align_bytes=64)
            scales = keep.tile([P, SLOTS], U8, name=f"x_scales{g}", align_bytes=64)
            quantise(codes[:], scales[:], grouped[:].rearrange("p w u -> p (w u)").bitcast(BF16))
            x_quantised[g] = (codes, scales)

        w1_quantised = {}

        def first_weights(e, g, parts):
            raw = raws["w1", e, g]
            grouped = ring.tile([P, H, J], BF16, name="w_grouped", bufs=3, align_bytes=64)
            for engine, lo, hi in parts:
                copy_on(
                    engine,
                    grouped[:].rearrange("p (t m) j -> p m j t", t=J)[:, lo:hi, :, :],
                    raw[:].rearrange("p j (m t) -> p m j t", t=J)[:, lo:hi, :, :],
                )
            codes = keep.tile([P, H], U32, name=f"w1_codes{e}_{g}", align_bytes=64)
            scales = keep.tile([P, H], U8, name=f"w1_scales{e}_{g}", align_bytes=64)
            quantise(codes[:], scales[:], grouped[:].rearrange("p w j -> p (w j)"))
            w1_quantised[e, g] = (codes, scales)

        w2_quantised = {}

        def second_weights(e, parts):
            raw = raws["w2", e]
            codes = keep.tile([P, N], U32, name=f"w2_codes{e}", align_bytes=64)
            scales = keep.tile([P, N], U8, name=f"w2_scales{e}", align_bytes=64)
            grouped = ring.tile([P, H, J], BF16, name="w_grouped", bufs=3, align_bytes=64)
            for engine, lo, hi in parts:
                copy_on(
                    engine,
                    grouped[:, lo:hi, :].rearrange("p (c i) t -> p c t i", i=4),
                    raw[:, :, lo:hi].rearrange("p t (c i) -> p c t i", i=4),
                )
            for lo, hi in ((0, 256), (256, 384)):
                quantise(codes[:, lo:hi], scales[:, lo:hi], grouped[:, lo:hi, :].rearrange("p w j -> p (w j)"))
            w2_quantised[e] = (codes, scales)

        results = {}

        def expert(e):
            hidden = []
            for s in range(C // HALF):
                slots = slice(e * C + s * HALF, e * C + (s + 1) * HALF)
                grouped = ring.tile([P, HALF, J], BF16, name="h_grouped", bufs=4, align_bytes=64)
                for q in range(0, J, 2):
                    acc = psum.tile([P, 2, HALF], F32, name="hidden_acc")
                    for t in range(q, q + 2):
                        rows = slice(t * P, (t + 1) * P)
                        for i, g in enumerate([[0,1,2],[0,1,2]][e]):
                            codes, scales = w1_quantised[e, g]
                            x_codes, x_scales = x_quantised[g]
                            nc.tensor.matmul_mx(
                                out=acc[:, t - q, :],
                                lhsT=codes[:, rows].bitcast(FP8X4),
                                lhsT_scale=scales[:, rows],
                                rhs=x_codes[:, slots].bitcast(FP8X4),
                                rhs_scale=x_scales[:, slots],
                                start=(i == 0),
                                stop=(i == PASSES - 1),
                            )
                    nc.scalar.activation(out=grouped[:, :, q : q + 2], in_=acc[:].rearrange("p t n -> p n t"), func=SILU)
                h_codes = ring.tile([P, HALF], U32, name="h_codes", bufs=4, align_bytes=64)
                h_scales = ring.tile([P, HALF], U8, name="h_scales", bufs=4, align_bytes=64)
                quantise(h_codes[:], h_scales[:], grouped[:].rearrange("p w j -> p (w j)"))
                hidden.append((h_codes, h_scales))
            codes, scales = w2_quantised[e]
            for n in range(FEATURE_BLOCKS):
                rows = slice(n * P, (n + 1) * P)
                acc = psum.tile([P, C], F32, name="result_acc")
                for s, (h_codes, h_scales) in enumerate(hidden):
                    nc.tensor.matmul_mx(
                        out=acc[:, s * HALF : (s + 1) * HALF],
                        lhsT=codes[:, rows].bitcast(FP8X4),
                        lhsT_scale=scales[:, rows],
                        rhs=h_codes[:].bitcast(FP8X4),
                        rhs_scale=h_scales[:],
                        start=True,
                        stop=True,
                    )
                result = ring.tile([P, C], F32, name="result", bufs=6)
                nc.scalar.copy(out=result[:], in_=acc[:])
                results[e, n] = result

        def scatter(e):
            for n in range(FEATURE_BLOCKS):
                nc.vector.tensor_tensor(
                    windows[n][:].indirect(lists[:, e * C // 16 : (e + 1) * C // 16]),
                    results[e, n][:],
                    gates[n][:, e * C : (e + 1) * C],
                    MULT,
                )

        gates = []
        for n in range(FEATURE_BLOCKS):
            gate_rows = keep.tile([P, SLOTS], F32, name=f"gates{n}")
            gates.append(gate_rows)

        def load_gate(n):
            nc.sync.dma_start(gates[n][:], gate[n * P : (n + 1) * P, :])

        load_pair(0, 0, 1)
        load_pair(0, 1, 1)
        load_pair(1, 0, 1)
        load_pair(1, 1, 1)
        load_pair(2, 0, 1)
        load_pair(2, 1, 1)
        load_w1(0, 0)
        load_w1(0, 1)
        load_w1(0, 2)
        load_w2(0)
        load_w1(1, 0)
        load_gate(0)
        load_w1(1, 1)
        load_gate(1)
        load_w1(1, 2)
        load_w2(1)
        load_gate(2)
        tokens_by_pairs(0, ([["S",0,768],["V",768,1536]], [["S",0,768],["V",768,1536]]))
        tokens_by_pairs(1, ([["S",0,768],["V",768,1536]], [["S",0,768],["V",768,1536]]))
        tokens_by_pairs(2, ([["S",0,768],["V",768,1536]], [["S",0,768],["V",768,1536]]))
        first_weights(0, 0, [["S",0,128]])
        first_weights(0, 1, [["S",0,64],["V",64,128]])
        first_weights(0, 2, [["S",0,64],["V",64,128]])
        second_weights(0, [["V",0,384]])
        expert(0)
        first_weights(1, 0, [["V",0,128]])
        first_weights(1, 1, [["S",0,64],["V",64,128]])
        first_weights(1, 2, [["S",0,128]])
        second_weights(1, [["S",0,288],["V",288,384]])
        expert(1)
        scatter(0)
        scatter(1)
        for n in range(FEATURE_BLOCKS):
            nc.sync.dma_start(out[n * P : (n + 1) * P, :], windows[n][:])
